import numpy as np, ml_dtypes
CORES = [22,38,54,62,70,110,23,39,55,63,71,111]
N = 12
TK = 512
def silu(z): return z / (1.0 + np.exp(-z))
def setup_inputs(rng):
    return {"x": rng.standard_normal((N, 128, TK), dtype=np.float32).astype(ml_dtypes.bfloat16), "w1": (rng.standard_normal((N, 128, 128), dtype=np.float32) / 8).astype(ml_dtypes.bfloat16), "w3": (rng.standard_normal((N, 128, 128), dtype=np.float32) / 8).astype(ml_dtypes.bfloat16), "w2": (rng.standard_normal((N, 128, 128), dtype=np.float32) / 8).astype(ml_dtypes.bfloat16)}
def setup_inputs_big(rng):
    d = setup_inputs(rng)
    for k in ("x",): d[k] = (d[k].astype(np.float32) * 1024.0).astype(d[k].dtype)
    return d
def setup_inputs_small(rng):
    d = setup_inputs(rng)
    for k in ("x",): d[k] = (d[k].astype(np.float32) * (1 / 1024.0)).astype(d[k].dtype)
    return d
def setup_inputs_apart(rng):
    d = setup_inputs(rng)
    f = (10.0 ** rng.permutation(np.linspace(-1.5, 1.5, N))).astype(np.float32).reshape(N, 1, 1)
    for k in ("x",): d[k] = (d[k].astype(np.float32) * f).astype(d[k].dtype)
    return d
def reference(x, w1, w3, w2):
    X, W1, W3, W2 = x.astype(np.float64), w1.astype(np.float64), w3.astype(np.float64), w2.astype(np.float64)
    y = np.zeros((N, 128, TK))
    for r in range(N):
        for j in range(N):
            y[r] += W2[j].T @ (silu(W1[j].T @ X[r]) * (W3[j].T @ X[r]))
    return {"y": y.astype(ml_dtypes.bfloat16)}

@@ -1,0 +1,293 @@
+from concourse.bass import DstId, RemoteDMATransfer
+from concourse.mybir import AluOpType, ActivationFunctionType
+
+N = 12
+TK = 512
+D = 128
+WS = 3 * D
+NH = 4
+NCH = 2
+W = TK // NCH
+NB = 2
+FWD = True
+ENG_OFF = 8
+ENG_ON = 8
+ENG_X = 8
+ENG_P = 8
+
+SCRATCH = {
+    "wbuf": ("sbuf", [128, N * WS], "bfloat16"),
+    "xbuf": ("sbuf", [128, 2 * TK], "bfloat16"),
+    "pbuf": ("sbuf", [128, max(NH, 1) * TK], "bfloat16"),
+    "pout": ("sbuf", [128, 2 * TK], "bfloat16"),
+    "yout": ("sbuf", [128, TK], "bfloat16"),
+    "ones": ("sbuf", [128, D], "bfloat16"),
+    "ident": ("sbuf", [128, D], "bfloat16"),
+}
+for _b in range(NB):
+    SCRATCH["sb%d" % _b] = ("sbuf", [128, W], "bfloat16")
+    SCRATCH["hb%d" % _b] = ("sbuf", [128, W], "bfloat16")
+    SCRATCH["z1_%d" % _b] = ("psum", [128, 512], "float32")
+    SCRATCH["z3_%d" % _b] = ("psum", [128, 512], "float32")
+for _b in range(2 * NCH):
+    SCRATCH["y_%d" % _b] = ("psum", [128, 512], "float32")
+
+SEMAPHORES = (["wld", "xld", "sent", "z1d", "z3d", "actd", "hd", "m2d", "cp0", "cp1", "std", "onesd", "idn",
+               "xa0", "xa1"] + ["w%d" % _j for _j in range(N)] + ["p%d" % _s for _s in range(max(NH, 1))])
+
+
+def _bits(m):
+    return [b for b in range(m.bit_length()) if (m >> b) & 1]
+
+
+def _pick(cands, n):
+    return sum(1 << b for b in cands[:n])
+
+
+def _plan(T, topo):
+    cores = list(T.cores)
+    chips = []
+    for c in cores:
+        if topo.chip(c) not in chips:
+            chips.append(topo.chip(c))
+    nq = len(chips)
+    ranks_on = [[c for c in cores if topo.chip(c) == ch] for ch in chips]
+    spare = []
+    for q, ch in enumerate(chips):
+        d = topo.die(ranks_on[q][0])
+        sp = [c for c in range(max(cores) + 1) if topo.chip(c) == ch and c not in cores]
+        sp.sort(key=lambda c: (topo.die(c) != d, c))
+        spare.append(sp[:NH])
+    gops = {}
+    units = {}
+    wcnt = {}
+    adds = {}
+    xest = {}
+    info = {}
+    for q in range(nq):
+        for l, c in enumerate(ranks_on[q]):
+            info[c] = (q, l, None)
+            gops[c], units[c], adds[c] = [], [], []
+            hs = spare[q]
+            cut = (l * len(hs)) // len(ranks_on[q])
+            order = hs[cut:] + hs[:cut]
+            for i, h in enumerate(order):
+                xest[(h, l)] = 8.0 + 0.8 * i
+            if order:
+                gops[c].append((2.02, "x", order))
+        for s, h in enumerate(spare[q]):
+            info[h] = (q, None, s)
+            gops[h], units[h] = [], []
+    for j, o in enumerate(cores):
+        q0, l, _ = info[o]
+        units[o].append((2.0, j, l))
+        off = []
+        for k in range(1, nq):
+            q = (q0 + k) % nq
+            est = 7.0 + 0.9 * k
+            idx = (k - 1) * len(ranks_on[q0]) + l
+            if idx < len(spare[q]):
+                h = spare[q][idx]
+                off.append(h)
+                wcnt[(j, h)] = ENG_OFF
+                toks = sorted(range(len(ranks_on[q])), key=lambda t: xest[(h, t)])
+                for i, t in enumerate(toks):
+                    units[h].append((est + i, j, t))
+                    gops[h].append((est + i, "p", t))
+                    adds[ranks_on[q][t]].append((max(est, xest[(h, toks[0])]) + 8.0 + i, idx))
+            else:
+                first = ranks_on[q][l % len(ranks_on[q])]
+                rest = [c for c in ranks_on[q] if c != first]
+                off.append(first)
+                wcnt[(j, first)] = ENG_OFF
+                units[first].append((est, j, info[first][1]))
+                for c in rest:
+                    if FWD:
+                        wcnt[(j, c)] = ENG_ON
+                        units[c].append((est + 3.0, j, info[c][1]))
+                    else:
+                        off.append(c)
+                        wcnt[(j, c)] = ENG_OFF
+                        units[c].append((est + 0.4, j, info[c][1]))
+                if FWD and rest:
+                    gops[first].append((est, "w", (j, rest)))
+        gops[o].append((2.0, "w", (j, off)))
+        mates_here = [c for c in ranks_on[q0] if c != o]
+        for c in mates_here:
+            wcnt[(j, c)] = ENG_ON
+            units[c].append((7.0, j, info[c][1]))
+        if mates_here:
+            gops[o].append((2.01, "w", (j, mates_here)))
+    for d in (gops, units, adds):
+        for c in d:
+            d[c].sort(key=lambda e: e[0])
+    return {"gops": gops, "units": units, "wcnt": wcnt, "adds": adds, "info": info, "ranks_on": ranks_on}
+
+
+def rank_program(g, core, T, topo):
+    P = _plan(T, topo)
+    if core not in P["info"]:
+        return
+    sem = T.sem
+    rank = T.rank_of(core)
+    q, letter, slot = P["info"][core]
+    pe, act, dve, sy = g.tensor, g.scalar, g.vector, g.sync
+    units = [(j, t) for (_, j, t) in P["units"][core]]
+    adds = [s for (_, s) in P["adds"].get(core, [])]
+
+    far = [c for c in T.cores if topo.chip(c) != topo.chip(core)][0]
+    near = [c for c in P["info"] if topo.chip(c) == topo.chip(core) and c != core][0]
+    off = _bits(topo.mask(core, far))
+    on = _bits(topo.mask(core, near))
+    hi = [b for b in on if b not in off]
+    m_off = _pick(off, ENG_OFF)
+    m_on = _pick(hi if len(hi) >= ENG_ON else on, ENG_ON)
+    m_x = _pick(hi if len(hi) >= ENG_X else on, ENG_X)
+    m_p = _pick(on[::2] if len(on[::2]) >= ENG_P else on, ENG_P)
+
+    if rank is not None:
+        c0 = rank * WS
+        sy.dma_start(T.wbuf[:, c0:c0 + D], T.w1[:]).then_inc(sem.wld, 16)
+        act.dma_start(T.wbuf[:, c0 + D:c0 + 2 * D], T.w3[:]).then_inc(sem.wld, 16)
+        sy.dma_start(T.wbuf[:, c0 + 2 * D:c0 + WS], T.w2[:]).then_inc(sem.wld, 16)
+        act.dma_start(T.xbuf[:, letter * TK:(letter + 1) * TK], T.x[:]).then_inc(sem.xld, 16)
+        if adds:
+            dve.memset(T.ones[:], 1.0).then_inc(sem.onesd, 1)
+            g.wait_ge(sem.onesd, 1)
+            g.affine_select(T.ident[:], T.ones[:], [[-1, D]], AluOpType.is_equal, 0.0, 0, 1).then_inc(sem.idn, 1)
+
+    sent = [0]
+
+    def write(src, dst, dsts, rsem, mask, neng):
+        if len(dsts) == 1:
+            rid, pid, _ = topo.addr(dsts[0])
+            g.remote_dma(out_ap=dst, in_ap=src, remote_sem=rsem, local_sem=sem.sent, pid=pid, routing_id=rid,
+                         dma_engine_mask=mask)
+        else:
+            ids = [DstId(rid=topo.addr(d)[0], pnc=topo.addr(d)[1]) for d in dsts]
+            g.remote_dma_fused([RemoteDMATransfer(dst_ids=ids, dma_engine_mask=mask, remote_sem=rsem, srcs=[src],
+                                                  dsts=[dst] * len(dsts), alu_op=0)], local_sem=sem.sent)
+        sent[0] += neng
+
+    waited = set()
+    for (_, kind, pay) in P["gops"][core]:
+        if kind == "w":
+            j, dsts = pay
+            if j not in waited:
+                waited.add(j)
+                if j == rank:
+                    g.wait_ge(sem.wld, 48)
+                else:
+                    g.wait_ge(sem["w%d" % j], P["wcnt"][(j, core)])
+            blk = T.wbuf[:, j * WS:(j + 1) * WS]
+            if topo.chip(dsts[0]) != topo.chip(core):
+                write(blk, blk, dsts, sem["w%d" % j], m_off, ENG_OFF)
+            else:
+                write(blk, blk, dsts, sem["w%d" % j], m_on, ENG_ON)
+        elif kind == "x":
+            g.wait_ge(sem.xld, 16)
+            blk = T.xbuf[:, letter * TK:(letter + 1) * TK]
+            write(blk, blk, pay, sem["xa%d" % letter], m_x, ENG_X)
+        else:
+            t = pay
+            g.wait_ge(sem["cp%d" % t], NCH)
+            write(T.pout[:, t * TK:(t + 1) * TK], T.pbuf[:, slot * TK:(slot + 1) * TK], [P["ranks_on"][q][t]],
+                  sem["p%d" % slot], m_p, ENG_P)
+    if sent[0]:
+        g.wait_ge(sem.sent, sent[0])
+
+    items = [(j, t, ch) for (j, t) in units for ch in range(NCH)]
+    n = len(items)
+    first, last = {}, {}
+    for i, (j, t, ch) in enumerate(items):
+        first.setdefault((t, ch), i)
+        last[(t, ch)] = i
+    z1 = [T["z1_%d" % b] for b in range(NB)]
+    z3 = [T["z3_%d" % b] for b in range(NB)]
+    sb = [T["sb%d" % b] for b in range(NB)]
+    hb = [T["hb%d" % b] for b in range(NB)]
+    yb = [T["y_%d" % b] for b in range(2 * NCH)]
+    seen_w, seen_x = set(), set()
+
+    def stage_a(i):
+        j, t, ch = items[i]
+        b = i % NB
+        if j not in seen_w:
+            seen_w.add(j)
+            if j == rank:
+                pe.wait_ge(sem.wld, 48)
+            else:
+                pe.wait_ge(sem["w%d" % j], P["wcnt"][(j, core)])
+        if t not in seen_x:
+            seen_x.add(t)
+            if rank is not None:
+                pe.wait_ge(sem.xld, 16)
+            else:
+                pe.wait_ge(sem["xa%d" % t], ENG_X)
+        if i >= NB:
+            pe.wait_ge(sem.actd, i - NB + 1)
+            pe.wait_ge(sem.hd, i - NB + 1)
+        xs = T.xbuf[:, t * TK + ch * W:t * TK + (ch + 1) * W]
+        pe.matmul(z1[b][:, 0:W], T.wbuf[:, j * WS:j * WS + D], xs, True, True).then_inc(sem.z1d, 1)
+        pe.matmul(z3[b][:, 0:W], T.wbuf[:, j * WS + D:j * WS + 2 * D], xs, True, True).then_inc(sem.z3d, 1)
+
+    def stage_b(i):
+        j, t, ch = items[i]
+        pe.wait_ge(sem.hd, i + 1)
+        pe.matmul(yb[t * NCH + ch][:, 0:W], T.wbuf[:, j * WS + 2 * D:(j + 1) * WS], hb[i % NB][:],
+                  first[(t, ch)] == i, last[(t, ch)] == i and not adds).then_inc(sem.m2d, 1)
+
+    for i in range(n + 1):
+        if i < n:
+            stage_a(i)
+        if i >= 1:
+            stage_b(i - 1)
+    done = {k: v + 1 for k, v in last.items()}
+    cnt = n
+    if adds:
+        pe.wait_ge(sem.idn, 1)
+        for a, s in enumerate(adds):
+            pe.wait_ge(sem["p%d" % s], ENG_P)
+            for ch in range(NCH):
+                pe.matmul(yb[letter * NCH + ch][:, 0:W], T.ident[:], T.pbuf[:, s * TK + ch * W:s * TK + (ch + 1) * W],
+                          False, a == len(adds) - 1).then_inc(sem.m2d, 1)
+                cnt += 1
+                done[(letter, ch)] = cnt
+
+    def copy_out(t, ch):
+        src = yb[t * NCH + ch][:, 0:W]
+        out = T.yout[:, ch * W:(ch + 1) * W] if rank is not None else T.pout[:, t * TK + ch * W:t * TK + (ch + 1) * W]
+        if ch % 2:
+            act.wait_ge(sem.m2d, done[(t, ch)])
+            act.activation(out, src, ActivationFunctionType.Copy).then_inc(sem["cp%d" % t], 1)
+        else:
+            dve.wait_ge(sem.m2d, done[(t, ch)])
+            dve.tensor_copy(out, src).then_inc(sem["cp%d" % t], 1)
+
+    pos = {k: (n if adds else min(v + 1, n)) for k, v in last.items()}
+    keys = sorted(last, key=lambda k: done[k])
+    for par in (1, 0):
+        for i in range(n):
+            b = i % NB
+            if par:
+                act.wait_ge(sem.z1d, i + 1)
+                if i >= NB:
+                    act.wait_ge(sem.hd, i - NB + 1)
+                act.activation(sb[b][:], z1[b][:, 0:W], ActivationFunctionType.Silu).then_inc(sem.actd, 1)
+            else:
+                dve.wait_ge(sem.actd, i + 1)
+                dve.wait_ge(sem.z3d, i + 1)
+                if i >= NB:
+                    dve.wait_ge(sem.m2d, i - NB + 1)
+                dve.tensor_tensor(hb[b][:], sb[b][:], z3[b][:, 0:W], AluOpType.mult).then_inc(sem.hd, 1)
+            for k in keys:
+                if k[1] % 2 == par and pos[k] == i:
+                    copy_out(k[0], k[1])
+        for k in keys:
+            if k[1] % 2 == par and pos[k] >= n:
+                copy_out(k[0], k[1])
+
+    if rank is not None:
+        sy.wait_ge(sem["cp%d" % letter], NCH)
+        sy.dma_start(T.y[:], T.yout[:]).then_inc(sem.std, 16)
+        sy.wait_ge(sem.std, 16)

@@ -5,7 +5,9 @@ N = 12
 TK = 512
 D = 128
 WS = 3 * D
-NH = 4
+NH = 6
+TWIN = True
+HFWD = True
 NCH = 2
 W = TK // NCH
 NB = 2
@@ -65,38 +67,62 @@ def _plan(T, topo):
     xest = {}
     info = {}
     for q in range(nq):
+        nl = len(ranks_on[q])
         for l, c in enumerate(ranks_on[q]):
-            info[c] = (q, l, None)
+            info[c] = (q, l)
             gops[c], units[c], adds[c] = [], [], []
             hs = spare[q]
-            cut = (l * len(hs)) // len(ranks_on[q])
-            order = hs[cut:] + hs[:cut]
+            if TWIN:
+                order = hs[l::nl]
+            else:
+                cut = (l * len(hs)) // nl
+                order = hs[cut:] + hs[:cut]
             for i, h in enumerate(order):
                 xest[(h, l)] = 8.0 + 0.8 * i
             if order:
                 gops[c].append((2.02, "x", order))
-        for s, h in enumerate(spare[q]):
-            info[h] = (q, None, s)
+        for h in spare[q]:
+            info[h] = (q, None)
             gops[h], units[h] = [], []
     for j, o in enumerate(cores):
-        q0, l, _ = info[o]
+        q0, l = info[o]
         units[o].append((2.0, j, l))
         off = []
         for k in range(1, nq):
             q = (q0 + k) % nq
+            nl = len(ranks_on[q])
             est = 7.0 + 0.9 * k
-            idx = (k - 1) * len(ranks_on[q0]) + l
-            if idx < len(spare[q]):
+            idx = (k - 1) * nl + l
+            if idx < len(spare[q]) and TWIN:
                 h = spare[q][idx]
                 off.append(h)
                 wcnt[(j, h)] = ENG_OFF
-                toks = sorted(range(len(ranks_on[q])), key=lambda t: xest[(h, t)])
+                units[h].append((est, j, l))
+                gops[h].append((est + 5.0, "p", (l, k - 1)))
+                adds[ranks_on[q][l]].append((est + 10.0, k - 1))
+                twins = [spare[q][(k - 1) * nl + m] for m in range(nl) if m != l]
+                for tw in twins:
+                    m = spare[q].index(tw) - (k - 1) * nl
+                    if HFWD:
+                        wcnt[(j, tw)] = ENG_ON
+                        units[tw].append((est + 4.0, j, m))
+                    else:
+                        off.append(tw)
+                        wcnt[(j, tw)] = ENG_OFF
+                        units[tw].append((est + 0.4, j, m))
+                if HFWD:
+                    gops[h].append((est, "w", (j, twins)))
+            elif idx < len(spare[q]):
+                h = spare[q][idx]
+                off.append(h)
+                wcnt[(j, h)] = ENG_OFF
+                toks = sorted(range(nl), key=lambda t: xest[(h, t)])
                 for i, t in enumerate(toks):
                     units[h].append((est + i, j, t))
-                    gops[h].append((est + i, "p", t))
+                    gops[h].append((est + i, "p", (t, idx)))
                     adds[ranks_on[q][t]].append((max(est, xest[(h, toks[0])]) + 8.0 + i, idx))
             else:
-                first = ranks_on[q][l % len(ranks_on[q])]
+                first = ranks_on[q][l % nl]
                 rest = [c for c in ranks_on[q] if c != first]
                 off.append(first)
                 wcnt[(j, first)] = ENG_OFF
@@ -130,7 +156,7 @@ def rank_program(g, core, T, topo):
         return
     sem = T.sem
     rank = T.rank_of(core)
-    q, letter, slot = P["info"][core]
+    q, letter = P["info"][core]
     pe, act, dve, sy = g.tensor, g.scalar, g.vector, g.sync
     units = [(j, t) for (_, j, t) in P["units"][core]]
     adds = [s for (_, s) in P["adds"].get(core, [])]
@@ -144,6 +170,8 @@ def rank_program(g, core, T, topo):
     m_on = _pick(hi if len(hi) >= ENG_ON else on, ENG_ON)
     m_x = _pick(hi if len(hi) >= ENG_X else on, ENG_X)
     m_p = _pick(on[::2] if len(on[::2]) >= ENG_P else on, ENG_P)
+    if rank is None and ENG_ON == ENG_P:
+        m_on = m_p
 
     if rank is not None:
         c0 = rank * WS
@@ -189,7 +217,7 @@ def rank_program(g, core, T, topo):
             blk = T.xbuf[:, letter * TK:(letter + 1) * TK]
             write(blk, blk, pay, sem["xa%d" % letter], m_x, ENG_X)
         else:
-            t = pay
+            t, slot = pay
             g.wait_ge(sem["cp%d" % t], NCH)
             write(T.pout[:, t * TK:(t + 1) * TK], T.pbuf[:, slot * TK:(slot + 1) * TK], [P["ranks_on"][q][t]],
                   sem["p%d" % slot], m_p, ENG_P)
@@ -237,11 +265,19 @@ def rank_program(g, core, T, topo):
         pe.matmul(yb[t * NCH + ch][:, 0:W], T.wbuf[:, j * WS + 2 * D:(j + 1) * WS], hb[i % NB][:],
                   first[(t, ch)] == i, last[(t, ch)] == i and not adds).then_inc(sem.m2d, 1)
 
-    for i in range(n + 1):
-        if i < n:
-            stage_a(i)
-        if i >= 1:
-            stage_b(i - 1)
+    nextb = 0
+    for i in range(n):
+        if rank is None and i > 0 and items[i][0] != items[i - 1][0]:
+            while nextb < i:
+                stage_b(nextb)
+                nextb += 1
+        stage_a(i)
+        while nextb < i:
+            stage_b(nextb)
+            nextb += 1
+    while nextb < n:
+        stage_b(nextb)
+        nextb += 1
     done = {k: v + 1 for k, v in last.items()}
     cnt = n
     if adds:

@@ -6,36 +6,32 @@ TK = 512
 D = 128
 WS = 3 * D
 NH = 6
-TWIN = True
-HFWD = True
+BND = [0, 176, 336, 512]
 NCH = 2
 W = TK // NCH
 NB = 2
-FWD = True
 ENG_OFF = 8
 ENG_ON = 8
 ENG_X = 8
-ENG_P = 8
+ENG_H = 16
 
 SCRATCH = {
     "wbuf": ("sbuf", [128, N * WS], "bfloat16"),
     "xbuf": ("sbuf", [128, 2 * TK], "bfloat16"),
-    "pbuf": ("sbuf", [128, max(NH, 1) * TK], "bfloat16"),
-    "pout": ("sbuf", [128, 2 * TK], "bfloat16"),
+    "pbuf": ("sbuf", [128, TK], "bfloat16"),
+    "pout": ("sbuf", [128, W], "bfloat16"),
     "yout": ("sbuf", [128, TK], "bfloat16"),
-    "ones": ("sbuf", [128, D], "bfloat16"),
-    "ident": ("sbuf", [128, D], "bfloat16"),
 }
 for _b in range(NB):
     SCRATCH["sb%d" % _b] = ("sbuf", [128, W], "bfloat16")
     SCRATCH["hb%d" % _b] = ("sbuf", [128, W], "bfloat16")
     SCRATCH["z1_%d" % _b] = ("psum", [128, 512], "float32")
     SCRATCH["z3_%d" % _b] = ("psum", [128, 512], "float32")
-for _b in range(2 * NCH):
+for _b in range(NCH):
     SCRATCH["y_%d" % _b] = ("psum", [128, 512], "float32")
 
-SEMAPHORES = (["wld", "xld", "sent", "z1d", "z3d", "actd", "hd", "m2d", "cp0", "cp1", "std", "onesd", "idn",
-               "xa0", "xa1"] + ["w%d" % _j for _j in range(N)] + ["p%d" % _s for _s in range(max(NH, 1))])
+SEMAPHORES = (["wld", "xld", "sent", "z1d", "z3d", "actd", "hd", "m2d", "cp0", "cp1", "std", "std2", "p0",
+               "xa0", "xa1"] + ["w%d" % _j for _j in range(N)])
 
 
 def _bits(m):
@@ -63,91 +59,61 @@ def _plan(T, topo):
     gops = {}
     units = {}
     wcnt = {}
-    adds = {}
-    xest = {}
     info = {}
+    nparts = {}
     for q in range(nq):
         nl = len(ranks_on[q])
         for l, c in enumerate(ranks_on[q]):
-            info[c] = (q, l)
-            gops[c], units[c], adds[c] = [], [], []
-            hs = spare[q]
-            if TWIN:
-                order = hs[l::nl]
-            else:
-                cut = (l * len(hs)) // nl
-                order = hs[cut:] + hs[:cut]
-            for i, h in enumerate(order):
-                xest[(h, l)] = 8.0 + 0.8 * i
-            if order:
-                gops[c].append((2.02, "x", order))
-        for h in spare[q]:
-            info[h] = (q, None)
-            gops[h], units[h] = [], []
+            info[c] = (q, l, None)
+            gops[c], units[c] = [], []
+            mine = spare[q][l::nl]
+            nparts[c] = len(mine)
+            for m, h in enumerate(mine):
+                gops[c].append((2.02 + 0.001 * m, "x", (h, m)))
+        for i, h in enumerate(spare[q]):
+            info[h] = (q, i % nl, i // nl)
+            gops[h], units[h] = [(99.0, "p", None)], []
     for j, o in enumerate(cores):
-        q0, l = info[o]
-        units[o].append((2.0, j, l))
+        q0, l, _ = info[o]
+        units[o].append((2.0, j))
         off = []
         for k in range(1, nq):
             q = (q0 + k) % nq
             nl = len(ranks_on[q])
             est = 7.0 + 0.9 * k
             idx = (k - 1) * nl + l
-            if idx < len(spare[q]) and TWIN:
+            if idx < len(spare[q]):
                 h = spare[q][idx]
                 off.append(h)
                 wcnt[(j, h)] = ENG_OFF
-                units[h].append((est, j, l))
-                gops[h].append((est + 5.0, "p", (l, k - 1)))
-                adds[ranks_on[q][l]].append((est + 10.0, k - 1))
-                twins = [spare[q][(k - 1) * nl + m] for m in range(nl) if m != l]
-                for tw in twins:
-                    m = spare[q].index(tw) - (k - 1) * nl
-                    if HFWD:
-                        wcnt[(j, tw)] = ENG_ON
-                        units[tw].append((est + 4.0, j, m))
-                    else:
-                        off.append(tw)
-                        wcnt[(j, tw)] = ENG_OFF
-                        units[tw].append((est + 0.4, j, m))
-                if HFWD:
-                    gops[h].append((est, "w", (j, twins)))
-            elif idx < len(spare[q]):
-                h = spare[q][idx]
-                off.append(h)
-                wcnt[(j, h)] = ENG_OFF
-                toks = sorted(range(nl), key=lambda t: xest[(h, t)])
-                for i, t in enumerate(toks):
-                    units[h].append((est + i, j, t))
-                    gops[h].append((est + i, "p", (t, idx)))
-                    adds[ranks_on[q][t]].append((max(est, xest[(h, toks[0])]) + 8.0 + i, idx))
+                units[h].append((est, j))
+                others = spare[q][idx + 1:] + spare[q][:idx]
+                for pos, tw in enumerate(others):
+                    wcnt[(j, tw)] = ENG_H
+                    units[tw].append((est + 3.0 + 0.5 * pos, j))
+                gops[h].append((est, "w", (j, others)))
             else:
                 first = ranks_on[q][l % nl]
                 rest = [c for c in ranks_on[q] if c != first]
                 off.append(first)
                 wcnt[(j, first)] = ENG_OFF
-                units[first].append((est, j, info[first][1]))
+                units[first].append((est, j))
                 for c in rest:
-                    if FWD:
-                        wcnt[(j, c)] = ENG_ON
-                        units[c].append((est + 3.0, j, info[c][1]))
-                    else:
-                        off.append(c)
-                        wcnt[(j, c)] = ENG_OFF
-                        units[c].append((est + 0.4, j, info[c][1]))
-                if FWD and rest:
+                    wcnt[(j, c)] = ENG_ON
+                    units[c].append((est + 3.0, j))
+                if rest:
                     gops[first].append((est, "w", (j, rest)))
         gops[o].append((2.0, "w", (j, off)))
         mates_here = [c for c in ranks_on[q0] if c != o]
         for c in mates_here:
             wcnt[(j, c)] = ENG_ON
-            units[c].append((7.0, j, info[c][1]))
+            units[c].append((7.0, j))
         if mates_here:
             gops[o].append((2.01, "w", (j, mates_here)))
-    for d in (gops, units, adds):
+    for d in (gops, units):
         for c in d:
             d[c].sort(key=lambda e: e[0])
-    return {"gops": gops, "units": units, "wcnt": wcnt, "adds": adds, "info": info, "ranks_on": ranks_on}
+    return {"gops": gops, "units": units, "wcnt": wcnt, "info": info, "ranks_on": ranks_on, "nparts": nparts}
 
 
 def rank_program(g, core, T, topo):
@@ -156,10 +122,9 @@ def rank_program(g, core, T, topo):
         return
     sem = T.sem
     rank = T.rank_of(core)
-    q, letter = P["info"][core]
+    q, letter, third = P["info"][core]
     pe, act, dve, sy = g.tensor, g.scalar, g.vector, g.sync
-    units = [(j, t) for (_, j, t) in P["units"][core]]
-    adds = [s for (_, s) in P["adds"].get(core, [])]
+    units = [j for (_, j) in P["units"][core]]
 
     far = [c for c in T.cores if topo.chip(c) != topo.chip(core)][0]
     near = [c for c in P["info"] if topo.chip(c) == topo.chip(core) and c != core][0]
@@ -169,9 +134,7 @@ def rank_program(g, core, T, topo):
     m_off = _pick(off, ENG_OFF)
     m_on = _pick(hi if len(hi) >= ENG_ON else on, ENG_ON)
     m_x = _pick(hi if len(hi) >= ENG_X else on, ENG_X)
-    m_p = _pick(on[::2] if len(on[::2]) >= ENG_P else on, ENG_P)
-    if rank is None and ENG_ON == ENG_P:
-        m_on = m_p
+    m_h = _pick(on, ENG_H)
 
     if rank is not None:
         c0 = rank * WS
@@ -179,10 +142,11 @@ def rank_program(g, core, T, topo):
         act.dma_start(T.wbuf[:, c0 + D:c0 + 2 * D], T.w3[:]).then_inc(sem.wld, 16)
         sy.dma_start(T.wbuf[:, c0 + 2 * D:c0 + WS], T.w2[:]).then_inc(sem.wld, 16)
         act.dma_start(T.xbuf[:, letter * TK:(letter + 1) * TK], T.x[:]).then_inc(sem.xld, 16)
-        if adds:
-            dve.memset(T.ones[:], 1.0).then_inc(sem.onesd, 1)
-            g.wait_ge(sem.onesd, 1)
-            g.affine_select(T.ident[:], T.ones[:], [[-1, D]], AluOpType.is_equal, 0.0, 0, 1).then_inc(sem.idn, 1)
+
+    if rank is not None:
+        blocks = [(letter * TK + ch * W, W) for ch in range(NCH)]
+    else:
+        blocks = [(letter * TK + BND[third], BND[third + 1] - BND[third])]
 
     sent = [0]
 
@@ -210,35 +174,37 @@ def rank_program(g, core, T, topo):
             blk = T.wbuf[:, j * WS:(j + 1) * WS]
             if topo.chip(dsts[0]) != topo.chip(core):
                 write(blk, blk, dsts, sem["w%d" % j], m_off, ENG_OFF)
+            elif rank is None:
+                write(blk, blk, dsts, sem["w%d" % j], m_h, ENG_H)
             else:
                 write(blk, blk, dsts, sem["w%d" % j], m_on, ENG_ON)
         elif kind == "x":
+            h, m = pay
             g.wait_ge(sem.xld, 16)
-            blk = T.xbuf[:, letter * TK:(letter + 1) * TK]
-            write(blk, blk, pay, sem["xa%d" % letter], m_x, ENG_X)
+            blk = T.xbuf[:, letter * TK + BND[m]:letter * TK + BND[m + 1]]
+            write(blk, blk, [h], sem["xa%d" % letter], m_x, ENG_X)
         else:
-            t, slot = pay
-            g.wait_ge(sem["cp%d" % t], NCH)
-            write(T.pout[:, t * TK:(t + 1) * TK], T.pbuf[:, slot * TK:(slot + 1) * TK], [P["ranks_on"][q][t]],
-                  sem["p%d" % slot], m_p, ENG_P)
+            g.wait_ge(sem.cp0, 1)
+            write(T.pout[:, 0:blocks[0][1]], T.pbuf[:, BND[third]:BND[third + 1]], [P["ranks_on"][q][letter]],
+                  sem.p0, m_h, ENG_H)
     if sent[0]:
         g.wait_ge(sem.sent, sent[0])
 
-    items = [(j, t, ch) for (j, t) in units for ch in range(NCH)]
+    items = [(j, x0, wd, yi) for j in units for yi, (x0, wd) in enumerate(blocks)]
     n = len(items)
     first, last = {}, {}
-    for i, (j, t, ch) in enumerate(items):
-        first.setdefault((t, ch), i)
-        last[(t, ch)] = i
+    for i, it in enumerate(items):
+        first.setdefault(it[3], i)
+        last[it[3]] = i
     z1 = [T["z1_%d" % b] for b in range(NB)]
     z3 = [T["z3_%d" % b] for b in range(NB)]
     sb = [T["sb%d" % b] for b in range(NB)]
     hb = [T["hb%d" % b] for b in range(NB)]
-    yb = [T["y_%d" % b] for b in range(2 * NCH)]
-    seen_w, seen_x = set(), set()
+    yb = [T["y_%d" % b] for b in range(NCH)]
+    seen_w = set()
 
     def stage_a(i):
-        j, t, ch = items[i]
+        j, x0, wd, yi = items[i]
         b = i % NB
         if j not in seen_w:
             seen_w.add(j)
@@ -246,84 +212,58 @@ def rank_program(g, core, T, topo):
                 pe.wait_ge(sem.wld, 48)
             else:
                 pe.wait_ge(sem["w%d" % j], P["wcnt"][(j, core)])
-        if t not in seen_x:
-            seen_x.add(t)
+        if i == 0:
             if rank is not None:
                 pe.wait_ge(sem.xld, 16)
             else:
-                pe.wait_ge(sem["xa%d" % t], ENG_X)
+                pe.wait_ge(sem["xa%d" % letter], ENG_X)
         if i >= NB:
             pe.wait_ge(sem.actd, i - NB + 1)
             pe.wait_ge(sem.hd, i - NB + 1)
-        xs = T.xbuf[:, t * TK + ch * W:t * TK + (ch + 1) * W]
-        pe.matmul(z1[b][:, 0:W], T.wbuf[:, j * WS:j * WS + D], xs, True, True).then_inc(sem.z1d, 1)
-        pe.matmul(z3[b][:, 0:W], T.wbuf[:, j * WS + D:j * WS + 2 * D], xs, True, True).then_inc(sem.z3d, 1)
+        xs = T.xbuf[:, x0:x0 + wd]
+        pe.matmul(z1[b][:, 0:wd], T.wbuf[:, j * WS:j * WS + D], xs, True, True).then_inc(sem.z1d, 1)
+        pe.matmul(z3[b][:, 0:wd], T.wbuf[:, j * WS + D:j * WS + 2 * D], xs, True, True).then_inc(sem.z3d, 1)
 
     def stage_b(i):
-        j, t, ch = items[i]
+        j, x0, wd, yi = items[i]
         pe.wait_ge(sem.hd, i + 1)
-        pe.matmul(yb[t * NCH + ch][:, 0:W], T.wbuf[:, j * WS + 2 * D:(j + 1) * WS], hb[i % NB][:],
-                  first[(t, ch)] == i, last[(t, ch)] == i and not adds).then_inc(sem.m2d, 1)
+        pe.matmul(yb[yi][:, 0:wd], T.wbuf[:, j * WS + 2 * D:(j + 1) * WS], hb[i % NB][:, 0:wd],
+                  first[yi] == i, last[yi] == i).then_inc(sem.m2d, 1)
 
-    nextb = 0
     for i in range(n):
-        if rank is None and i > 0 and items[i][0] != items[i - 1][0]:
-            while nextb < i:
-                stage_b(nextb)
-                nextb += 1
         stage_a(i)
-        while nextb < i:
-            stage_b(nextb)
-            nextb += 1
-    while nextb < n:
-        stage_b(nextb)
-        nextb += 1
-    done = {k: v + 1 for k, v in last.items()}
-    cnt = n
-    if adds:
-        pe.wait_ge(sem.idn, 1)
-        for a, s in enumerate(adds):
-            pe.wait_ge(sem["p%d" % s], ENG_P)
-            for ch in range(NCH):
-                pe.matmul(yb[letter * NCH + ch][:, 0:W], T.ident[:], T.pbuf[:, s * TK + ch * W:s * TK + (ch + 1) * W],
-                          False, a == len(adds) - 1).then_inc(sem.m2d, 1)
-                cnt += 1
-                done[(letter, ch)] = cnt
+        if i > 0:
+            stage_b(i - 1)
+    stage_b(n - 1)
 
-    def copy_out(t, ch):
-        src = yb[t * NCH + ch][:, 0:W]
-        out = T.yout[:, ch * W:(ch + 1) * W] if rank is not None else T.pout[:, t * TK + ch * W:t * TK + (ch + 1) * W]
-        if ch % 2:
-            act.wait_ge(sem.m2d, done[(t, ch)])
-            act.activation(out, src, ActivationFunctionType.Copy).then_inc(sem["cp%d" % t], 1)
+    for i, (j, x0, wd, yi) in enumerate(items):
+        b = i % NB
+        act.wait_ge(sem.z1d, i + 1)
+        if i >= NB:
+            act.wait_ge(sem.hd, i - NB + 1)
+        act.activation(sb[b][:, 0:wd], z1[b][:, 0:wd], ActivationFunctionType.Silu).then_inc(sem.actd, 1)
+
+    for i, (j, x0, wd, yi) in enumerate(items):
+        b = i % NB
+        dve.wait_ge(sem.actd, i + 1)
+        dve.wait_ge(sem.z3d, i + 1)
+        if i >= NB:
+            dve.wait_ge(sem.m2d, i - NB + 1)
+        dve.tensor_tensor(hb[b][:, 0:wd], sb[b][:, 0:wd], z3[b][:, 0:wd], AluOpType.mult).then_inc(sem.hd, 1)
+    for yi, (x0, wd) in enumerate(blocks):
+        dve.wait_ge(sem.m2d, last[yi] + 1)
+        if rank is not None:
+            if yi == 0:
+                dve.wait_ge(sem.p0, P["nparts"][core] * ENG_H)
+            dve.tensor_tensor(T.yout[:, yi * W:(yi + 1) * W], yb[yi][:, 0:W], T.pbuf[:, yi * W:(yi + 1) * W],
+                              AluOpType.add).then_inc(sem["cp%d" % yi], 1)
         else:
-            dve.wait_ge(sem.m2d, done[(t, ch)])
-            dve.tensor_copy(out, src).then_inc(sem["cp%d" % t], 1)
-
-    pos = {k: (n if adds else min(v + 1, n)) for k, v in last.items()}
-    keys = sorted(last, key=lambda k: done[k])
-    for par in (1, 0):
-        for i in range(n):
-            b = i % NB
-            if par:
-                act.wait_ge(sem.z1d, i + 1)
-                if i >= NB:
-                    act.wait_ge(sem.hd, i - NB + 1)
-                act.activation(sb[b][:], z1[b][:, 0:W], ActivationFunctionType.Silu).then_inc(sem.actd, 1)
-            else:
-                dve.wait_ge(sem.actd, i + 1)
-                dve.wait_ge(sem.z3d, i + 1)
-                if i >= NB:
-                    dve.wait_ge(sem.m2d, i - NB + 1)
-                dve.tensor_tensor(hb[b][:], sb[b][:], z3[b][:, 0:W], AluOpType.mult).then_inc(sem.hd, 1)
-            for k in keys:
-                if k[1] % 2 == par and pos[k] == i:
-                    copy_out(k[0], k[1])
-        for k in keys:
-            if k[1] % 2 == par and pos[k] >= n:
-                copy_out(k[0], k[1])
+            dve.tensor_copy(T.pout[:, 0:wd], yb[yi][:, 0:wd]).then_inc(sem.cp0, 1)
 
     if rank is not None:
-        sy.wait_ge(sem["cp%d" % letter], NCH)
-        sy.dma_start(T.y[:], T.yout[:]).then_inc(sem.std, 16)
+        sy.wait_ge(sem.cp0, 1)
+        sy.dma_start(T.y[:, 0:W], T.yout[:, 0:W]).then_inc(sem.std, 16)
         sy.wait_ge(sem.std, 16)
+        act.wait_ge(sem.cp1, 1)
+        act.dma_start(T.y[:, W:TK], T.yout[:, W:TK]).then_inc(sem.std2, 16)
+        act.wait_ge(sem.std2, 16)

@@ -9,7 +9,8 @@ NH = 6
 BND = [0, 176, 336, 512]
 NCH = 2
 W = TK // NCH
-NB = 2
+NB = 3
+LAG = 2
 ENG_OFF = 8
 ENG_ON = 8
 ENG_X = 8
@@ -59,20 +60,25 @@ def _plan(T, topo):
     gops = {}
     units = {}
     wcnt = {}
+    xcnt = {}
     info = {}
     nparts = {}
     for q in range(nq):
         nl = len(ranks_on[q])
+        for i, h in enumerate(spare[q]):
+            info[h] = (q, i % nl, i // nl)
+            gops[h], units[h] = [(99.0, "p", None)], []
         for l, c in enumerate(ranks_on[q]):
             info[c] = (q, l, None)
             gops[c], units[c] = [], []
             mine = spare[q][l::nl]
             nparts[c] = len(mine)
-            for m, h in enumerate(mine):
-                gops[c].append((2.02 + 0.001 * m, "x", (h, m)))
-        for i, h in enumerate(spare[q]):
-            info[h] = (q, i % nl, i // nl)
-            gops[h], units[h] = [(99.0, "p", None)], []
+            root = mine[-1]
+            gops[c].append((2.005, "x", root))
+            xcnt[root] = ENG_X
+            for m, h in enumerate(mine[:-1]):
+                gops[root].append((5.0 + 0.001 * m, "xf", (h, m)))
+                xcnt[h] = ENG_H
     for j, o in enumerate(cores):
         q0, l, _ = info[o]
         units[o].append((2.0, j))
@@ -113,7 +119,8 @@ def _plan(T, topo):
     for d in (gops, units):
         for c in d:
             d[c].sort(key=lambda e: e[0])
-    return {"gops": gops, "units": units, "wcnt": wcnt, "info": info, "ranks_on": ranks_on, "nparts": nparts}
+    return {"gops": gops, "units": units, "wcnt": wcnt, "xcnt": xcnt, "info": info, "ranks_on": ranks_on,
+            "nparts": nparts}
 
 
 def rank_program(g, core, T, topo):
@@ -179,10 +186,14 @@ def rank_program(g, core, T, topo):
             else:
                 write(blk, blk, dsts, sem["w%d" % j], m_on, ENG_ON)
         elif kind == "x":
-            h, m = pay
             g.wait_ge(sem.xld, 16)
+            blk = T.xbuf[:, letter * TK:(letter + 1) * TK]
+            write(blk, blk, [pay], sem["xa%d" % letter], m_x, ENG_X)
+        elif kind == "xf":
+            h, m = pay
+            g.wait_ge(sem["xa%d" % letter], P["xcnt"][core])
             blk = T.xbuf[:, letter * TK + BND[m]:letter * TK + BND[m + 1]]
-            write(blk, blk, [h], sem["xa%d" % letter], m_x, ENG_X)
+            write(blk, blk, [h], sem["xa%d" % letter], m_h, ENG_H)
         else:
             g.wait_ge(sem.cp0, 1)
             write(T.pout[:, 0:blocks[0][1]], T.pbuf[:, BND[third]:BND[third + 1]], [P["ranks_on"][q][letter]],
@@ -216,7 +227,7 @@ def rank_program(g, core, T, topo):
             if rank is not None:
                 pe.wait_ge(sem.xld, 16)
             else:
-                pe.wait_ge(sem["xa%d" % letter], ENG_X)
+                pe.wait_ge(sem["xa%d" % letter], P["xcnt"][core])
         if i >= NB:
             pe.wait_ge(sem.actd, i - NB + 1)
             pe.wait_ge(sem.hd, i - NB + 1)
@@ -230,11 +241,15 @@ def rank_program(g, core, T, topo):
         pe.matmul(yb[yi][:, 0:wd], T.wbuf[:, j * WS + 2 * D:(j + 1) * WS], hb[i % NB][:, 0:wd],
                   first[yi] == i, last[yi] == i).then_inc(sem.m2d, 1)
 
+    nextb = 0
     for i in range(n):
         stage_a(i)
-        if i > 0:
-            stage_b(i - 1)
-    stage_b(n - 1)
+        if i >= LAG:
+            stage_b(nextb)
+            nextb += 1
+    while nextb < n:
+        stage_b(nextb)
+        nextb += 1
 
     for i, (j, x0, wd, yi) in enumerate(items):
         b = i % NB

from concourse.bass import DstId, RemoteDMATransfer
from concourse.mybir import AluOpType, ActivationFunctionType

N = 12
TK = 512
D = 128
WS = 3 * D
NH = 6
BND = [0, 176, 336, 512]
NCH = 2
W = TK // NCH
NB = 3
LAG = 2
ENG_OFF = 8
ENG_ON = 8
ENG_X = 8
ENG_H = 16

SCRATCH = {
    "wbuf": ("sbuf", [128, N * WS], "bfloat16"),
    "xbuf": ("sbuf", [128, 2 * TK], "bfloat16"),
    "pbuf": ("sbuf", [128, TK], "bfloat16"),
    "pout": ("sbuf", [128, W], "bfloat16"),
    "yout": ("sbuf", [128, TK], "bfloat16"),
}
for _b in range(NB):
    SCRATCH["sb%d" % _b] = ("sbuf", [128, W], "bfloat16")
    SCRATCH["hb%d" % _b] = ("sbuf", [128, W], "bfloat16")
    SCRATCH["z1_%d" % _b] = ("psum", [128, 512], "float32")
    SCRATCH["z3_%d" % _b] = ("psum", [128, 512], "float32")
for _b in range(NCH):
    SCRATCH["y_%d" % _b] = ("psum", [128, 512], "float32")

SEMAPHORES = (["wld", "xld", "sent", "z1d", "z3d", "actd", "hd", "m2d", "cp0", "cp1", "std", "std2", "p0",
               "xa0", "xa1"] + ["w%d" % _j for _j in range(N)])


def _bits(m):
    return [b for b in range(m.bit_length()) if (m >> b) & 1]


def _pick(cands, n):
    return sum(1 << b for b in cands[:n])


def _plan(T, topo):
    cores = list(T.cores)
    chips = []
    for c in cores:
        if topo.chip(c) not in chips:
            chips.append(topo.chip(c))
    nq = len(chips)
    ranks_on = [[c for c in cores if topo.chip(c) == ch] for ch in chips]
    spare = []
    for q, ch in enumerate(chips):
        d = topo.die(ranks_on[q][0])
        sp = [c for c in range(max(cores) + 1) if topo.chip(c) == ch and c not in cores]
        sp.sort(key=lambda c: (topo.die(c) != d, c))
        spare.append(sp[:NH])
    gops = {}
    units = {}
    wcnt = {}
    xcnt = {}
    info = {}
    nparts = {}
    for q in range(nq):
        nl = len(ranks_on[q])
        for i, h in enumerate(spare[q]):
            info[h] = (q, i % nl, i // nl)
            gops[h], units[h] = [(99.0, "p", None)], []
        for l, c in enumerate(ranks_on[q]):
            info[c] = (q, l, None)
            gops[c], units[c] = [], []
            mine = spare[q][l::nl]
            nparts[c] = len(mine)
            root = mine[-1]
            gops[c].append((2.005, "x", root))
            xcnt[root] = ENG_X
            for m, h in enumerate(mine[:-1]):
                gops[root].append((5.0 + 0.001 * m, "xf", (h, m)))
                xcnt[h] = ENG_H
    for j, o in enumerate(cores):
        q0, l, _ = info[o]
        units[o].append((2.0, j))
        off = []
        for k in range(1, nq):
            q = (q0 + k) % nq
            nl = len(ranks_on[q])
            est = 7.0 + 0.9 * k
            idx = (k - 1) * nl + l
            if idx < len(spare[q]):
                h = spare[q][idx]
                off.append(h)
                wcnt[(j, h)] = ENG_OFF
                units[h].append((est, j))
                others = spare[q][idx + 1:] + spare[q][:idx]
                for pos, tw in enumerate(others):
                    wcnt[(j, tw)] = ENG_H
                    units[tw].append((est + 3.0 + 0.5 * pos, j))
                gops[h].append((est, "w", (j, others)))
            else:
                first = ranks_on[q][l % nl]
                rest = [c for c in ranks_on[q] if c != first]
                off.append(first)
                wcnt[(j, first)] = ENG_OFF
                units[first].append((est, j))
                for c in rest:
                    wcnt[(j, c)] = ENG_ON
                    units[c].append((est + 3.0, j))
                if rest:
                    gops[first].append((est, "w", (j, rest)))
        gops[o].append((2.0, "w", (j, off)))
        mates_here = [c for c in ranks_on[q0] if c != o]
        for c in mates_here:
            wcnt[(j, c)] = ENG_ON
            units[c].append((7.0, j))
        if mates_here:
            gops[o].append((2.01, "w", (j, mates_here)))
    for d in (gops, units):
        for c in d:
            d[c].sort(key=lambda e: e[0])
    return {"gops": gops, "units": units, "wcnt": wcnt, "xcnt": xcnt, "info": info, "ranks_on": ranks_on,
            "nparts": nparts}


def rank_program(g, core, T, topo):
    P = _plan(T, topo)
    if core not in P["info"]:
        return
    sem = T.sem
    rank = T.rank_of(core)
    q, letter, third = P["info"][core]
    pe, act, dve, sy = g.tensor, g.scalar, g.vector, g.sync
    units = [j for (_, j) in P["units"][core]]

    far = [c for c in T.cores if topo.chip(c) != topo.chip(core)][0]
    near = [c for c in P["info"] if topo.chip(c) == topo.chip(core) and c != core][0]
    off = _bits(topo.mask(core, far))
    on = _bits(topo.mask(core, near))
    hi = [b for b in on if b not in off]
    m_off = _pick(off, ENG_OFF)
    m_on = _pick(hi if len(hi) >= ENG_ON else on, ENG_ON)
    m_x = _pick(hi if len(hi) >= ENG_X else on, ENG_X)
    m_h = _pick(on, ENG_H)

    if rank is not None:
        c0 = rank * WS
        sy.dma_start(T.wbuf[:, c0:c0 + D], T.w1[:]).then_inc(sem.wld, 16)
        act.dma_start(T.wbuf[:, c0 + D:c0 + 2 * D], T.w3[:]).then_inc(sem.wld, 16)
        sy.dma_start(T.wbuf[:, c0 + 2 * D:c0 + WS], T.w2[:]).then_inc(sem.wld, 16)
        act.dma_start(T.xbuf[:, letter * TK:(letter + 1) * TK], T.x[:]).then_inc(sem.xld, 16)

    if rank is not None:
        blocks = [(letter * TK + ch * W, W) for ch in range(NCH)]
    else:
        blocks = [(letter * TK + BND[third], BND[third + 1] - BND[third])]

    sent = [0]

    def write(src, dst, dsts, rsem, mask, neng):
        if len(dsts) == 1:
            rid, pid, _ = topo.addr(dsts[0])
            g.remote_dma(out_ap=dst, in_ap=src, remote_sem=rsem, local_sem=sem.sent, pid=pid, routing_id=rid,
                         dma_engine_mask=mask)
        else:
            ids = [DstId(rid=topo.addr(d)[0], pnc=topo.addr(d)[1]) for d in dsts]
            g.remote_dma_fused([RemoteDMATransfer(dst_ids=ids, dma_engine_mask=mask, remote_sem=rsem, srcs=[src],
                                                  dsts=[dst] * len(dsts), alu_op=0)], local_sem=sem.sent)
        sent[0] += neng

    waited = set()
    for (_, kind, pay) in P["gops"][core]:
        if kind == "w":
            j, dsts = pay
            if j not in waited:
                waited.add(j)
                if j == rank:
                    g.wait_ge(sem.wld, 48)
                else:
                    g.wait_ge(sem["w%d" % j], P["wcnt"][(j, core)])
            blk = T.wbuf[:, j * WS:(j + 1) * WS]
            if topo.chip(dsts[0]) != topo.chip(core):
                write(blk, blk, dsts, sem["w%d" % j], m_off, ENG_OFF)
            elif rank is None:
                write(blk, blk, dsts, sem["w%d" % j], m_h, ENG_H)
            else:
                write(blk, blk, dsts, sem["w%d" % j], m_on, ENG_ON)
        elif kind == "x":
            g.wait_ge(sem.xld, 16)
            blk = T.xbuf[:, letter * TK:(letter + 1) * TK]
            write(blk, blk, [pay], sem["xa%d" % letter], m_x, ENG_X)
        elif kind == "xf":
            h, m = pay
            g.wait_ge(sem["xa%d" % letter], P["xcnt"][core])
            blk = T.xbuf[:, letter * TK + BND[m]:letter * TK + BND[m + 1]]
            write(blk, blk, [h], sem["xa%d" % letter], m_h, ENG_H)
        else:
            g.wait_ge(sem.cp0, 1)
            write(T.pout[:, 0:blocks[0][1]], T.pbuf[:, BND[third]:BND[third + 1]], [P["ranks_on"][q][letter]],
                  sem.p0, m_h, ENG_H)
    if sent[0]:
        g.wait_ge(sem.sent, sent[0])

    items = [(j, x0, wd, yi) for j in units for yi, (x0, wd) in enumerate(blocks)]
    n = len(items)
    first, last = {}, {}
    for i, it in enumerate(items):
        first.setdefault(it[3], i)
        last[it[3]] = i
    z1 = [T["z1_%d" % b] for b in range(NB)]
    z3 = [T["z3_%d" % b] for b in range(NB)]
    sb = [T["sb%d" % b] for b in range(NB)]
    hb = [T["hb%d" % b] for b in range(NB)]
    yb = [T["y_%d" % b] for b in range(NCH)]
    seen_w = set()

    def stage_a(i):
        j, x0, wd, yi = items[i]
        b = i % NB
        if j not in seen_w:
            seen_w.add(j)
            if j == rank:
                pe.wait_ge(sem.wld, 48)
            else:
                pe.wait_ge(sem["w%d" % j], P["wcnt"][(j, core)])
        if i == 0:
            if rank is not None:
                pe.wait_ge(sem.xld, 16)
            else:
                pe.wait_ge(sem["xa%d" % letter], P["xcnt"][core])
        if i >= NB:
            pe.wait_ge(sem.actd, i - NB + 1)
            pe.wait_ge(sem.hd, i - NB + 1)
        xs = T.xbuf[:, x0:x0 + wd]
        pe.matmul(z1[b][:, 0:wd], T.wbuf[:, j * WS:j * WS + D], xs, True, True).then_inc(sem.z1d, 1)
        pe.matmul(z3[b][:, 0:wd], T.wbuf[:, j * WS + D:j * WS + 2 * D], xs, True, True).then_inc(sem.z3d, 1)

    def stage_b(i):
        j, x0, wd, yi = items[i]
        pe.wait_ge(sem.hd, i + 1)
        pe.matmul(yb[yi][:, 0:wd], T.wbuf[:, j * WS + 2 * D:(j + 1) * WS], hb[i % NB][:, 0:wd],
                  first[yi] == i, last[yi] == i).then_inc(sem.m2d, 1)

    nextb = 0
    for i in range(n):
        stage_a(i)
        if i >= LAG:
            stage_b(nextb)
            nextb += 1
    while nextb < n:
        stage_b(nextb)
        nextb += 1

    for i, (j, x0, wd, yi) in enumerate(items):
        b = i % NB
        act.wait_ge(sem.z1d, i + 1)
        if i >= NB:
            act.wait_ge(sem.hd, i - NB + 1)
        act.activation(sb[b][:, 0:wd], z1[b][:, 0:wd], ActivationFunctionType.Silu).then_inc(sem.actd, 1)

    for i, (j, x0, wd, yi) in enumerate(items):
        b = i % NB
        dve.wait_ge(sem.actd, i + 1)
        dve.wait_ge(sem.z3d, i + 1)
        if i >= NB:
            dve.wait_ge(sem.m2d, i - NB + 1)
        dve.tensor_tensor(hb[b][:, 0:wd], sb[b][:, 0:wd], z3[b][:, 0:wd], AluOpType.mult).then_inc(sem.hd, 1)
    for yi, (x0, wd) in enumerate(blocks):
        dve.wait_ge(sem.m2d, last[yi] + 1)
        if rank is not None:
            if yi == 0:
                dve.wait_ge(sem.p0, P["nparts"][core] * ENG_H)
            dve.tensor_tensor(T.yout[:, yi * W:(yi + 1) * W], yb[yi][:, 0:W], T.pbuf[:, yi * W:(yi + 1) * W],
                              AluOpType.add).then_inc(sem["cp%d" % yi], 1)
        else:
            dve.tensor_copy(T.pout[:, 0:wd], yb[yi][:, 0:wd]).then_inc(sem.cp0, 1)

    if rank is not None:
        sy.wait_ge(sem.cp0, 1)
        sy.dma_start(T.y[:, 0:W], T.yout[:, 0:W]).then_inc(sem.std, 16)
        sy.wait_ge(sem.std, 16)
        act.wait_ge(sem.cp1, 1)
        act.dma_start(T.y[:, W:TK], T.yout[:, W:TK]).then_inc(sem.std2, 16)
        act.wait_ge(sem.std2, 16)
